import numpy as np
import ml_dtypes


def mxq(x, axis, fmt="e4m3"):
    dtype, down = {"e4m3": (ml_dtypes.float8_e4m3fn, 7), "e5m2": (ml_dtypes.float8_e5m2, 14)}[fmt]
    v = np.moveaxis(np.asarray(x, np.float32).astype(ml_dtypes.bfloat16).astype(np.float64), axis, -1)
    blocks = v.reshape(v.shape[:-1] + (-1, 32))
    amax = np.abs(blocks).max(-1, keepdims=True)
    byte = np.maximum(np.where(amax > 0, np.frexp(amax)[1] - 1 + 127, 0) - down, 1)
    scale = np.exp2(byte - 127.0)
    codes = (blocks / scale).astype(np.float32).astype(dtype).astype(np.float64)
    return np.moveaxis((codes * scale).reshape(v.shape), -1, axis)


WIDE = False


def mx_kscale(k):
    if not WIDE:
        return np.ones(k)
    levels = np.array([10, -10, 5, -5, 0])
    if k % 512:
        return np.exp2(np.random.permutation(np.resize(levels, k // 32))).repeat(32)
    a = np.empty((k // 512, 16))
    for p in range(k // 512):
        a[p, :8] = np.random.permutation(np.resize(levels, 8))
        for g in range(8):
            far = levels[np.abs(levels - a[p, g]) >= 10]
            a[p, g + 8] = far[np.random.randint(len(far))]
    return np.exp2(a.ravel()).repeat(32)


def f64(x):
    return np.asarray(x).astype(np.float64)


def striped(idx):
    return np.tile(np.asarray(idx).reshape(-1, 16).T, (8, 1)).astype(np.uint16)


def unstriped(offs):
    return offs[:16].T.reshape(-1).astype(np.int64)


E2M1 = np.array([0.0, 0.5, 1.0, 1.5, 2.0, 3.0, 4.0, 6.0, -0.0, -0.5, -1.0, -1.5, -2.0, -3.0, -4.0, -6.0])


def pack_weight(w, fmt):
    k, n = w.shape
    w = f64(np.asarray(w, np.float32).astype(ml_dtypes.bfloat16)).reshape(k // 32, 32, n)
    amax = np.abs(w).max(1)
    if fmt == "e4m3":
        byte = np.frexp(amax)[1] - 1 + 127 - 7
    else:
        mant, ex = np.frexp(amax / 6.0)
        byte = np.where(mant > 0.5, ex, ex - 1) + 127
    byte = np.clip(np.where(amax > 0, byte, 1), 1, 254)
    scaled = (w * np.exp2(127.0 - byte)[:, None, :]).reshape(k, n).astype(np.float32)
    by_word = np.ascontiguousarray(scaled.reshape(k // 512, 128, 4, n).transpose(0, 1, 3, 2))
    if fmt == "e4m3":
        words = by_word.astype(ml_dtypes.float8_e4m3fn).view(np.uint8)
    else:
        c = by_word.astype(ml_dtypes.float4_e2m1fn).view(np.uint8) & 0xF
        words = (c[..., 0::2] | (c[..., 1::2] << 4)).reshape(k // 512, 128, 2 * n)
    return np.ascontiguousarray(words), np.ascontiguousarray(byte.astype(np.uint8).reshape(k // 512, 16, n))


def unpack_weight(words, scales, fmt):
    g, _, n = scales.shape
    words = np.ascontiguousarray(words).reshape(g, 128, n, -1)
    if fmt == "e4m3":
        vals = words.view(ml_dtypes.float8_e4m3fn).astype(np.float64)
    else:
        nib = np.empty((g, 128, n, 4), np.uint8)
        nib[..., 0::2] = words & 0xF
        nib[..., 1::2] = words >> 4
        vals = E2M1[nib]
    vals = vals * np.repeat(np.exp2(scales.astype(np.float64) - 127.0), 8, axis=1)[..., None]
    return vals.transpose(0, 1, 3, 2).reshape(g * 512, n)


def sigmoid(v):
    return 1.0 / (1.0 + np.exp(-v))


D, E, T, I, Q, G = 512, 512, 2048, 512, 128, 32


def setup_inputs():
    n = np.random.standard_normal
    idx = np.random.permutation(T)[:I]
    fd = mx_kscale(D)
    fe = mx_kscale(E)
    fi = mx_kscale(I)
    ti = np.ones(T)
    ti[idx] = fi
    keysp = pack_weight(n((D, T)) / fd[:, None], "e2m1")
    valsp = pack_weight(n((E, T)) / fe[:, None], "e2m1")
    return {
        "query": (n((D, Q)) * 0.7 / np.sqrt(D) * fd[:, None]).astype(np.float32),
        "keys_words": keysp[0],
        "keys_scales": keysp[1],
        "th": (np.random.uniform(-0.2, 0.2, (Q, 1))).astype(np.float32),
        "steep": (np.random.uniform(2.0, 8.0, (Q, 1))).astype(np.float32),
        "gout": (n((E, Q)) * 1 / np.sqrt(E) * fe[:, None]).astype(np.float32),
        "vals_words": valsp[0],
        "vals_scales": valsp[1],
        "size": (np.random.uniform(0.5, 2.0, (1, I))).astype(np.float32),
        "dquery": (n((D, Q)) * 1.0 / np.sqrt(D) * fd[:, None]).astype(np.float32),
        "fs": (np.random.uniform(128.0, 512.0, (1, I)) * fi).astype(np.float32),
        "keyrows": (n((D, T)) / ti).astype(np.float32),
        "res": (n((Q, D)) * 4.0).astype(np.float32),
        "offs": striped(idx),
    }


def reference(query, keys_words, keys_scales, th, steep, gout, vals_words, vals_scales, size, dquery, fs, keyrows, res, offs):
    idx = unstriped(offs)
    keysu = unpack_weight(keys_words, keys_scales, "e2m1")
    valsu = unpack_weight(vals_words, vals_scales, "e2m1")
    queryq = mxq(f64(query), 0, "e4m3")
    keysidxg = keysu[:, idx]
    a = queryq.T @ keysidxg
    dqueryq = mxq(f64(dquery), 0, "e4m3")
    ta = dqueryq.T @ keysidxg
    s = a.reshape(Q, G, I // G).mean(axis=2)
    gt = sigmoid((s - f64(th)) * f64(steep))
    gr = np.repeat(gt, I // G, axis=1)
    r = np.exp(a - np.max(a, axis=1, keepdims=True))
    p = r * gr
    z = np.sum(p, axis=1, keepdims=True)
    goutq = mxq(f64(gout), 0, "e4m3")
    valsidxg = valsu[:, idx]
    c0 = goutq.T @ valsidxg
    dz = np.sum(c0 * p * f64(size) / np.square(z) * (-1.0), axis=1, keepdims=True)
    dp = c0 / z * f64(size) + dz
    dr = dp * gr
    dgr = dp * r
    dgt = dgr.reshape(Q, G, I // G).sum(axis=2)
    ts = ta.reshape(Q, G, I // G).mean(axis=2)
    tgt = ts * f64(steep) * gt * (1.0 - gt)
    tgr = np.repeat(tgt, I // G, axis=1)
    tr = ta * r
    tp = tr * gr + tgr * r
    tz = np.sum(tp, axis=1, keepdims=True)
    tdz = np.sum((tp * f64(size) * c0 - tz * z * 2.0 * c0 * p * f64(size) / np.square(z)) / np.square(z) * (-1.0), axis=1, keepdims=True)
    tdp = tz * c0 / np.square(z) * (-1.0) * f64(size) + tdz
    tdr = tdp * gr + tgr * dp
    tdgr = tdp * r + tr * dp
    tdgt = tdgr.reshape(Q, G, I // G).sum(axis=2)
    tds = ((tdgt * gt + tgt * dgt) * (1.0 - gt) + tgt * (-1.0) * dgt * gt) * f64(steep)
    te1 = tds / 16.0
    tr1 = np.repeat(te1, I // G, axis=1)
    tda = tdr * r + tr * dr + tr1
    gs = tda * f64(fs)
    gt1 = gs.T
    kt = f64(keyrows)[:, idx].T
    gt1q = mxq(gt1, 0, "e4m3")
    ktq = mxq(kt, 0, "e4m3")
    gq = gt1q.T @ ktq
    y = gq + f64(res)
    return y

@@ -1,0 +1,254 @@
+from contextlib import ExitStack
+
+import concourse.mybir as mybir
+from concourse.masks import make_identity
+
+D, E, T, SLOTS, Q, PAGES = 512, 512, 2048, 512, 128, 32
+FLOPS = 2 * Q * SLOTS * (2 * D + E) + 2 * Q * SLOTS * D
+
+P = 128
+PACK = 4
+PAGE = SLOTS // PAGES
+F32 = mybir.dt.float32
+BF16 = mybir.dt.bfloat16
+I32 = mybir.dt.int32
+U32 = mybir.dt.uint32
+U16 = mybir.dt.uint16
+U8 = mybir.dt.uint8
+FP8X4 = mybir.dt.float8_e4m3fn_x4
+FP4X4 = mybir.dt.float4_e2m1fn_x4
+ALU = mybir.AluOpType
+ACT = mybir.ActivationFunctionType
+AX = mybir.AxisListType
+EXP_CAP = 1.0e30
+SCALAR_BLOCKS = 2
+
+
+def tile_attend_hvpagegate_q_kernel(tc, query, keys_words, keys_scales, th, steep, gout, vals_words, vals_scales,
+                                     size, dquery, fs, keyrows, res, offs, out):
+    nc = tc.nc
+    with ExitStack() as ctx:
+        sb = ctx.enter_context(tc.tile_pool(name="sb", bufs=1))
+        ps = ctx.enter_context(tc.psum_pool(name="ps", bufs=1))
+
+        def sbt(name, shape, dtype, tag=None):
+            return sb.tile(shape, dtype, name=name, tag=tag or name, align_bytes=64)
+
+        def by_page(t):
+            return t[:].unsqueeze(1).unsqueeze(3).broadcast_to([P, PACK, PAGES, PACK])
+
+        def by_quarter_page(t):
+            return t[:].unsqueeze(2).broadcast_to([P, PAGES, PACK])
+
+        def dealt(bank):
+            return bank[:].rearrange("q (m t) -> q t m", t=PACK)
+
+        def pages_of(t):
+            return t[:].rearrange("q t (g u) -> q g t u", u=PACK)
+
+        def four(t):
+            return t.rearrange("q t (g u) -> q t g u", u=PACK)
+
+        offsets = sb.tile([P, SLOTS // 16], U16, name="offsets")
+        k_words = sbt("k_words", [P, T], U16)
+        k_scales = sbt("k_scales", [P, T], U8)
+        v_words = sbt("v_words", [P, T], U16)
+        v_scales = sbt("v_scales", [P, T], U8)
+        nc.vector.memset(k_scales[:].bitcast(I32), 0)
+        nc.vector.memset(v_scales[:].bitcast(I32), 0)
+        warm = sbt("warm", [P, 1], F32)
+        nc.vector.memset(warm[:], 0.0)
+        warm2 = sbt("warm2", [P, 1], F32)
+        nc.scalar.activation(warm2[:], warm[:], ACT.Exp)
+
+        def load_rows(name, src):
+            raw = sbt(name, [P, PACK, Q], F32)
+            nc.sync.dma_start(out=raw[:], in_=src.rearrange("(p j) q -> p j q", j=PACK))
+            return raw
+
+        def load_scales(plane, src):
+            for r in range(4):
+                nc.sync.dma_start(out=plane[r:P:32, :].bitcast(I32), in_=src[0, r:16:4, :].bitcast(I32))
+
+        nc.sync.dma_start(offsets[:], offs)
+        nc.sync.dma_start(out=k_words[:].bitcast(I32), in_=keys_words[0].bitcast(I32))
+        q_raw = load_rows("q_raw", query)
+        dq_raw = load_rows("dq_raw", dquery)
+        load_scales(k_scales, keys_scales)
+        steep_c = sbt("steep_c", [P, 1], F32)
+        th_c = sbt("th_c", [P, 1], F32)
+        size_c = sbt("size_c", [P, PACK], F32)
+        fs_c = sbt("fs_c", [P, PACK], F32)
+        rows = [sbt("rows%d" % j, [P, T], F32) for j in range(D // P)]
+
+        def load_block(j):
+            nc.sync.dma_start(out=rows[j][:], in_=keyrows[j * P:(j + 1) * P, :])
+
+        nc.sync.dma_start(out=v_words[:].bitcast(I32), in_=vals_words[0].bitcast(I32))
+        go_raw = load_rows("go_raw", gout)
+        load_block(0)
+        load_scales(v_scales, vals_scales)
+        for j in range(1, D // P):
+            load_block(j)
+        res_sb = sbt("res_sb", [P, D], F32)
+        nc.sync.dma_start(out=res_sb[:], in_=res)
+        nc.gpsimd.dma_start(out=th_c[:], in_=th)
+        nc.gpsimd.dma_start(out=steep_c[:], in_=steep)
+        ident = sbt("ident", [P, P], F32)
+        make_identity(nc, ident[:])
+        nc.gpsimd.dma_start(out=size_c[:], in_=size.rearrange("o (m t) -> (o m) t", t=PACK))
+        nc.gpsimd.dma_start(out=fs_c[:], in_=fs.rearrange("o (m t) -> (o m) t", t=PACK))
+
+        def quantise_rows(name, raw):
+            woven = sbt(name + "_woven", [P, Q, PACK], BF16)
+            nc.scalar.copy(woven[:], raw[:].rearrange("p j q -> p q j"))
+            codes = sbt(name + "_codes", [P, Q], U32)
+            plane = sbt(name + "_plane", [P, Q], U8)
+            nc.vector.quantize_mx(out=codes[:].bitcast(FP8X4), scales=plane[:],
+                                  in_=woven[:].rearrange("p q j -> p (q j)"))
+            return codes, plane
+
+        def gather(name, window, dtype, tag=None):
+            got = sbt(name, [P, SLOTS], dtype, tag)
+            nc.vector.tensor_copy(got[:], window[:].indirect(offsets[:]))
+            return got
+
+        def score(name, rows_mx, words, plane):
+            bank = ps.tile([P, SLOTS], F32, name=name)
+            nc.tensor.matmul_mx(out=bank[:], lhsT=rows_mx[0][:].bitcast(FP8X4), lhsT_scale=rows_mx[1][:],
+                                rhs=words[:].bitcast(FP4X4), rhs_scale=plane[:], start=True, stop=True)
+            return bank
+
+        kg_words = gather("kg_words", k_words, U16)
+        kg_scales = gather("kg_scales", k_scales, U8)
+        q_mx = quantise_rows("q", q_raw)
+        dq_mx = quantise_rows("dq", dq_raw)
+        a = score("a", q_mx, kg_words, kg_scales)
+        ta = score("ta", dq_mx, kg_words, kg_scales)
+        vg_words = gather("vg_words", v_words, U16, "q_woven")
+        vg_scales = gather("vg_scales", v_scales, U8, "dq_woven")
+        go_mx = quantise_rows("go", go_raw)
+        c0 = score("c0", go_mx, vg_words, vg_scales)
+
+        def col(name):
+            return sbt(name, [P, 1], F32)
+
+        def pag(name):
+            return sbt(name, [P, PAGES], F32)
+
+        def full(name):
+            return sbt(name, [P, PACK, P], F32)
+
+        kt_in = sbt("kt_in", [P, D, PACK], BF16)
+        kt_codes = sbt("kt_codes", [P, D], U32)
+        kt_plane = sbt("kt_plane", [P, D], U8)
+
+        def cast_block(j):
+            cast = sbt("rows_bf%d" % j, [P, T], BF16, "nmax" if j == 0 else None)
+            for c5 in range(0, T, 512):
+                nc.scalar.activation(cast[:, c5:c5 + 512], rows[j][:, c5:c5 + 512], ACT.Copy)
+            return cast
+
+        def pick_block(j, cast):
+            got = sbt("rows_g%d" % j, [P, SLOTS], BF16)
+            for c8 in range(0, SLOTS // 16, 16):
+                nc.scalar.activation(got[:, c8 * 16:(c8 + 16) * 16], cast[:].indirect(offsets[:, c8:c8 + 16]), ACT.Copy)
+            return got
+
+        def turn_block(j, got):
+            words = got[:].bitcast(F32)
+            turned = ps.tile([P, 2, P], F32, name="turned", bufs=2)
+            for u in range(2):
+                nc.tensor.transpose(turned[:, u, :], words[:, u:SLOTS // 2:2], ident[:])
+            nc.scalar.copy(kt_in[:, j * P:(j + 1) * P, :].bitcast(F32), turned[:].rearrange("p u d -> p d u"))
+            if j % 2 == 1:
+                cols = slice((j - 1) * P, (j + 1) * P)
+                nc.vector.quantize_mx(out=kt_codes[:, cols].bitcast(FP8X4), scales=kt_plane[:, cols],
+                                      in_=kt_in[:, cols, :].rearrange("p d t -> p (d t)"))
+
+        sa, sta, nmax = pag("sa"), pag("sta"), col("nmax")
+        nc.vector.tensor_reduce(sa[:], a[:].rearrange("q (g j) -> q g j", j=PAGE), AX.X, ALU.add)
+        nc.vector.tensor_reduce(nmax[:], a[:], AX.X, ALU.max, negate=True)
+        short, e = pag("short"), pag("e")
+        nc.scalar.activation(short[:], sa[:], ACT.Identity, bias=th_c[:], scale=-1.0 / PAGE)
+        nc.scalar.activation(e[:], short[:], ACT.Exp, scale=steep_c[:])
+        r = full("r")
+        nc.scalar.activation(r[:], dealt(a), ACT.Exp, bias=nmax[:])
+        size_b = ps.tile([P, PACK, P], F32, name="size_b", tag="a")
+        for t in range(PACK):
+            nc.tensor.transpose(size_b[:, t, :], size_c[:, t:t + 1].to_broadcast([P, P]), ident[:])
+        size_sb = full("size_sb")
+        nc.scalar.copy(size_sb[:], size_b[:])
+        for j in range(SCALAR_BLOCKS):
+            turn_block(j, pick_block(j, cast_block(j)))
+        den, gt = pag("den"), pag("gt")
+        nc.vector.tensor_scalar(den[:], e[:], EXP_CAP, 1.0, ALU.min, ALU.add)
+        nc.vector.tensor_reduce(sta[:], ta[:].rearrange("q (g j) -> q g j", j=PAGE), AX.X, ALU.add)
+        nc.vector.reciprocal(gt[:], den[:])
+        r_page = pag("r_page")
+        nc.vector.tensor_reduce(r_page[:], pages_of(r), AX.XY, ALU.add)
+        kn, hn, ln, pn_page, nz, niz, gn = pag("kn"), pag("hn"), pag("ln"), pag("pn_page"), col("nz"), col("niz"), pag("gn")
+        nc.vector.tensor_scalar(kn[:], gt[:], 1.0, steep_c[:], ALU.subtract, ALU.mult)
+        nc.vector.scalar_tensor_tensor(pn_page[:], r_page[:], -1.0, gt[:], ALU.mult, ALU.mult, accum_out=nz[:])
+        nc.vector.scalar_tensor_tensor(hn[:], sta[:], 1.0 / PAGE, kn[:], ALU.mult, ALU.mult)
+        nc.vector.reciprocal(niz[:], nz[:])
+        nc.vector.scalar_tensor_tensor(ln[:], hn[:], steep_c[:], gt[:], ALU.mult, ALU.mult)
+        nc.vector.tensor_scalar(gn[:], gt[:], niz[:], None, ALU.mult)
+        vn = full("vn")
+        nc.vector.tensor_tensor(four(vn[:]), by_page(hn), four(dealt(ta)), ALU.subtract)
+        pin = full("pin")
+        nc.vector.tensor_tensor(four(pin[:]), four(r[:]), by_page(gn), ALU.mult)
+        turn_block(2, gather("rows_g2", rows[2], BF16, "r"))
+        c = full("c")
+        nc.vector.tensor_tensor(c[:], dealt(c0), size_sb[:], ALU.mult)
+        pv, tau = full("pv"), col("tau")
+        nc.vector.scalar_tensor_tensor(pv[:], pin[:], 1.0, vn[:], ALU.mult, ALU.mult, accum_out=tau[:])
+        pcn, ns1 = full("pcn"), col("ns1")
+        nc.vector.scalar_tensor_tensor(pcn[:], pin[:], 1.0, c[:], ALU.mult, ALU.mult, accum_out=ns1[:])
+        turn_block(3, gather("rows_g3", rows[3], BF16, "vn"))
+        mass, kpn, mu = pag("mass"), pag("kpn"), pag("mu")
+        nc.scalar.activation(mass[:], pn_page[:], ACT.Copy, scale=niz[:])
+        nc.vector.scalar_tensor_tensor(mu[:], kn[:], tau[:], ln[:], ALU.mult, ALU.add)
+        pcn_page = pag("pcn_page")
+        nc.vector.tensor_reduce(pcn_page[:], pages_of(pcn), AX.XY, ALU.add)
+        x, cov = full("x"), col("cov")
+        nc.vector.scalar_tensor_tensor(x[:], c[:], ns1[:], pv[:], ALU.add, ALU.mult, accum_out=cov[:])
+        y_page, pre, x_page = pag("y_page"), pag("pre"), pag("x_page")
+        nc.vector.scalar_tensor_tensor(y_page[:], mass[:], ns1[:], pcn_page[:], ALU.mult, ALU.subtract)
+        nc.vector.scalar_tensor_tensor(kpn[:], mass[:], 1.0 / PAGE, kn[:], ALU.mult, ALU.mult)
+        nc.vector.scalar_tensor_tensor(pre[:], y_page[:], 1.0 / PAGE, mu[:], ALU.mult, ALU.mult)
+        nc.vector.tensor_reduce(x_page[:], pages_of(x), AX.XY, ALU.add)
+        tns, term_c, term_s, term_cov = col("tns"), full("term_c"), full("term_s"), full("term_cov")
+        nc.scalar.activation(tns[:], ns1[:], ACT.Copy, scale=tau[:])
+        nc.scalar.activation(term_c[:], pcn[:], ACT.Copy, scale=tau[:])
+        nc.scalar.activation(term_s[:], pin[:], ACT.Copy, scale=tns[:])
+        nc.scalar.activation(term_cov[:], pin[:], ACT.Copy, scale=cov[:])
+        early = sbt("early", [P, PAGES, PACK], F32)
+        late = sbt("late", [P, PAGES, PACK], F32)
+        nc.vector.scalar_tensor_tensor(early[:], by_quarter_page(kpn), cov[:], by_quarter_page(pre), ALU.mult, ALU.add)
+        nc.vector.scalar_tensor_tensor(late[:], by_quarter_page(x_page), -1.0 / PAGE, by_quarter_page(kn), ALU.mult, ALU.mult)
+
+        g_t = ps.tile([P, PACK, Q], F32, name="g_t")
+        terms = [lambda t: term_c[:, t, :], lambda t: term_s[:, t, :], lambda t: x[:, t, :],
+                 lambda t: term_cov[:, t, :],
+                 lambda t: early[:].rearrange("q g u -> q (g u)"), lambda t: late[:].rearrange("q g u -> q (g u)")]
+        for n, term in enumerate(terms):
+            for t in range(PACK):
+                nc.tensor.matmul(g_t[:, t, :], term(t), ident[:], is_transpose=True,
+                                 start=(n == 0 and t == 0), stop=(n == len(terms) - 1 and t == PACK - 1))
+        g_in = sbt("g_in", [P, Q, PACK], BF16)
+        nc.vector.tensor_tensor(g_in[:], g_t[:].rearrange("p t q -> p q t"),
+                                fs_c[:].unsqueeze(1).broadcast_to([P, Q, PACK]), ALU.mult)
+        g_codes = sbt("g_codes", [P, Q], U32)
+        g_plane = sbt("g_plane", [P, Q], U8)
+        nc.vector.quantize_mx(out=g_codes[:].bitcast(FP8X4), scales=g_plane[:], in_=g_in[:].rearrange("p q t -> p (q t)"))
+
+        half = D // 2
+        for h, tag in enumerate(("a", "ta")):
+            cols = slice(h * half, (h + 1) * half)
+            acc = ps.tile([P, half], F32, name="acc%d" % h, tag=tag)
+            nc.tensor.matmul_mx(out=acc[:], lhsT=g_codes[:].bitcast(FP8X4), lhsT_scale=g_plane[:],
+                                rhs=kt_codes[:, cols].bitcast(FP8X4), rhs_scale=kt_plane[:, cols], start=True, stop=True)
+            done = sbt("done%d" % h, [P, half], F32)
+            nc.vector.tensor_tensor(done[:], acc[:], res_sb[:, cols], ALU.add)
+            nc.sync.dma_start(out=out[:, cols], in_=done[:])

@@ -20,8 +20,7 @@ FP4X4 = mybir.dt.float4_e2m1fn_x4
 ALU = mybir.AluOpType
 ACT = mybir.ActivationFunctionType
 AX = mybir.AxisListType
-EXP_CAP = 1.0e30
-SCALAR_BLOCKS = 2
+SCALAR_BLOCKS = 1
 
 
 def tile_attend_hvpagegate_q_kernel(tc, query, keys_words, keys_scales, th, steep, gout, vals_words, vals_scales,
@@ -85,28 +84,30 @@ def tile_attend_hvpagegate_q_kernel(tc, query, keys_words, keys_scales, th, stee
             nc.sync.dma_start(out=rows[j][:], in_=keyrows[j * P:(j + 1) * P, :])
 
         nc.sync.dma_start(out=v_words[:].bitcast(I32), in_=vals_words[0].bitcast(I32))
+        nc.sync.dma_start(out=th_c[:], in_=th)
+        nc.sync.dma_start(out=steep_c[:], in_=steep)
         go_raw = load_rows("go_raw", gout)
-        load_block(0)
         load_scales(v_scales, vals_scales)
+        load_block(0)
+        nc.sync.dma_start(out=size_c[:], in_=size.rearrange("o (m t) -> (o m) t", t=PACK))
         for j in range(1, D // P):
             load_block(j)
+        nc.sync.dma_start(out=fs_c[:], in_=fs.rearrange("o (m t) -> (o m) t", t=PACK))
         res_sb = sbt("res_sb", [P, D], F32)
         nc.sync.dma_start(out=res_sb[:], in_=res)
-        nc.gpsimd.dma_start(out=th_c[:], in_=th)
-        nc.gpsimd.dma_start(out=steep_c[:], in_=steep)
         ident = sbt("ident", [P, P], F32)
         make_identity(nc, ident[:])
-        nc.gpsimd.dma_start(out=size_c[:], in_=size.rearrange("o (m t) -> (o m) t", t=PACK))
-        nc.gpsimd.dma_start(out=fs_c[:], in_=fs.rearrange("o (m t) -> (o m) t", t=PACK))
 
-        def quantise_rows(name, raw):
-            woven = sbt(name + "_woven", [P, Q, PACK], BF16)
-            nc.scalar.copy(woven[:], raw[:].rearrange("p j q -> p q j"))
-            codes = sbt(name + "_codes", [P, Q], U32)
-            plane = sbt(name + "_plane", [P, Q], U8)
+        def quantise_rows(name, raws):
+            n = len(raws)
+            woven = sbt(name + "_woven", [P, n * Q, PACK], BF16)
+            for i, raw in enumerate(raws):
+                nc.scalar.copy(woven[:, i * Q:(i + 1) * Q, :], raw[:].rearrange("p j q -> p q j"))
+            codes = sbt(name + "_codes", [P, n * Q], U32)
+            plane = sbt(name + "_plane", [P, n * Q], U8)
             nc.vector.quantize_mx(out=codes[:].bitcast(FP8X4), scales=plane[:],
                                   in_=woven[:].rearrange("p q j -> p (q j)"))
-            return codes, plane
+            return [(codes[:, i * Q:(i + 1) * Q], plane[:, i * Q:(i + 1) * Q]) for i in range(n)]
 
         def gather(name, window, dtype, tag=None):
             got = sbt(name, [P, SLOTS], dtype, tag)
@@ -115,20 +116,15 @@ def tile_attend_hvpagegate_q_kernel(tc, query, keys_words, keys_scales, th, stee
 
         def score(name, rows_mx, words, plane):
             bank = ps.tile([P, SLOTS], F32, name=name)
-            nc.tensor.matmul_mx(out=bank[:], lhsT=rows_mx[0][:].bitcast(FP8X4), lhsT_scale=rows_mx[1][:],
+            nc.tensor.matmul_mx(out=bank[:], lhsT=rows_mx[0].bitcast(FP8X4), lhsT_scale=rows_mx[1],
                                 rhs=words[:].bitcast(FP4X4), rhs_scale=plane[:], start=True, stop=True)
             return bank
 
         kg_words = gather("kg_words", k_words, U16)
         kg_scales = gather("kg_scales", k_scales, U8)
-        q_mx = quantise_rows("q", q_raw)
-        dq_mx = quantise_rows("dq", dq_raw)
+        q_mx, dq_mx = quantise_rows("q", [q_raw, dq_raw])
         a = score("a", q_mx, kg_words, kg_scales)
         ta = score("ta", dq_mx, kg_words, kg_scales)
-        vg_words = gather("vg_words", v_words, U16, "q_woven")
-        vg_scales = gather("vg_scales", v_scales, U8, "dq_woven")
-        go_mx = quantise_rows("go", go_raw)
-        c0 = score("c0", go_mx, vg_words, vg_scales)
 
         def col(name):
             return sbt(name, [P, 1], F32)
@@ -139,20 +135,16 @@ def tile_attend_hvpagegate_q_kernel(tc, query, keys_words, keys_scales, th, stee
         def full(name):
             return sbt(name, [P, PACK, P], F32)
 
-        kt_in = sbt("kt_in", [P, D, PACK], BF16)
-        kt_codes = sbt("kt_codes", [P, D], U32)
-        kt_plane = sbt("kt_plane", [P, D], U8)
+        kt_in = [sbt("kt_in%d" % h, [P, D // 2, PACK], BF16) for h in range(2)]
 
         def cast_block(j):
-            cast = sbt("rows_bf%d" % j, [P, T], BF16, "nmax" if j == 0 else None)
-            for c5 in range(0, T, 512):
-                nc.scalar.activation(cast[:, c5:c5 + 512], rows[j][:, c5:c5 + 512], ACT.Copy)
+            cast = sbt("rows_bf%d" % j, [P, T], BF16, "nmax")
+            nc.scalar.activation(cast[:], rows[j][:], ACT.Copy)
             return cast
 
         def pick_block(j, cast):
             got = sbt("rows_g%d" % j, [P, SLOTS], BF16)
-            for c8 in range(0, SLOTS // 16, 16):
-                nc.scalar.activation(got[:, c8 * 16:(c8 + 16) * 16], cast[:].indirect(offsets[:, c8:c8 + 16]), ACT.Copy)
+            nc.scalar.activation(got[:], cast[:].indirect(offsets[:]), ACT.Copy)
             return got
 
         def turn_block(j, got):
@@ -160,20 +152,22 @@ def tile_attend_hvpagegate_q_kernel(tc, query, keys_words, keys_scales, th, stee
             turned = ps.tile([P, 2, P], F32, name="turned", bufs=2)
             for u in range(2):
                 nc.tensor.transpose(turned[:, u, :], words[:, u:SLOTS // 2:2], ident[:])
-            nc.scalar.copy(kt_in[:, j * P:(j + 1) * P, :].bitcast(F32), turned[:].rearrange("p u d -> p d u"))
-            if j % 2 == 1:
-                cols = slice((j - 1) * P, (j + 1) * P)
-                nc.vector.quantize_mx(out=kt_codes[:, cols].bitcast(FP8X4), scales=kt_plane[:, cols],
-                                      in_=kt_in[:, cols, :].rearrange("p d t -> p (d t)"))
+            nc.scalar.copy(kt_in[j // 2][:, (j % 2) * P:(j % 2 + 1) * P, :].bitcast(F32), turned[:].rearrange("p u d -> p d u"))
 
+        vg_words = gather("vg_words", v_words, U16, "q_woven")
+        (go_mx,) = quantise_rows("go", [go_raw])
         sa, sta, nmax = pag("sa"), pag("sta"), col("nmax")
         nc.vector.tensor_reduce(sa[:], a[:].rearrange("q (g j) -> q g j", j=PAGE), AX.X, ALU.add)
         nc.vector.tensor_reduce(nmax[:], a[:], AX.X, ALU.max, negate=True)
         short, e = pag("short"), pag("e")
+        den = pag("den")
         nc.scalar.activation(short[:], sa[:], ACT.Identity, bias=th_c[:], scale=-1.0 / PAGE)
         nc.scalar.activation(e[:], short[:], ACT.Exp, scale=steep_c[:])
+        nc.scalar.activation(den[:], e[:], ACT.Copy, bias=1.0)
         r = full("r")
         nc.scalar.activation(r[:], dealt(a), ACT.Exp, bias=nmax[:])
+        vg_scales = gather("vg_scales", v_scales, U8, "sa")
+        c0 = score("c0", go_mx, vg_words, vg_scales)
         size_b = ps.tile([P, PACK, P], F32, name="size_b", tag="a")
         for t in range(PACK):
             nc.tensor.transpose(size_b[:, t, :], size_c[:, t:t + 1].to_broadcast([P, P]), ident[:])
@@ -181,67 +175,77 @@ def tile_attend_hvpagegate_q_kernel(tc, query, keys_words, keys_scales, th, stee
         nc.scalar.copy(size_sb[:], size_b[:])
         for j in range(SCALAR_BLOCKS):
             turn_block(j, pick_block(j, cast_block(j)))
-        den, gt = pag("den"), pag("gt")
-        nc.vector.tensor_scalar(den[:], e[:], EXP_CAP, 1.0, ALU.min, ALU.add)
+        gt = pag("gt")
         nc.vector.tensor_reduce(sta[:], ta[:].rearrange("q (g j) -> q g j", j=PAGE), AX.X, ALU.add)
         nc.vector.reciprocal(gt[:], den[:])
         r_page = pag("r_page")
         nc.vector.tensor_reduce(r_page[:], pages_of(r), AX.XY, ALU.add)
-        kn, hn, ln, pn_page, nz, niz, gn = pag("kn"), pag("hn"), pag("ln"), pag("pn_page"), col("nz"), col("niz"), pag("gn")
+        kn, hn, lean, pn_page, nz, niz = pag("kn"), pag("hn"), pag("lean"), pag("pn_page"), col("nz"), col("niz")
         nc.vector.tensor_scalar(kn[:], gt[:], 1.0, steep_c[:], ALU.subtract, ALU.mult)
-        nc.vector.scalar_tensor_tensor(pn_page[:], r_page[:], -1.0, gt[:], ALU.mult, ALU.mult, accum_out=nz[:])
+        p = full("p")
+        nc.vector.tensor_tensor(four(p[:]), four(r[:]), by_page(gt), ALU.mult)
         nc.vector.scalar_tensor_tensor(hn[:], sta[:], 1.0 / PAGE, kn[:], ALU.mult, ALU.mult)
-        nc.vector.reciprocal(niz[:], nz[:])
-        nc.vector.scalar_tensor_tensor(ln[:], hn[:], steep_c[:], gt[:], ALU.mult, ALU.mult)
-        nc.vector.tensor_scalar(gn[:], gt[:], niz[:], None, ALU.mult)
+        nc.vector.scalar_tensor_tensor(pn_page[:], r_page[:], -1.0, gt[:], ALU.mult, ALU.mult, accum_out=nz[:])
+        nc.vector.scalar_tensor_tensor(lean[:], sta[:], steep_c[:], gt[:], ALU.mult, ALU.mult)
         vn = full("vn")
         nc.vector.tensor_tensor(four(vn[:]), by_page(hn), four(dealt(ta)), ALU.subtract)
-        pin = full("pin")
-        nc.vector.tensor_tensor(four(pin[:]), four(r[:]), by_page(gn), ALU.mult)
-        turn_block(2, gather("rows_g2", rows[2], BF16, "r"))
+        nc.vector.reciprocal(niz[:], nz[:])
+        turn_block(1, gather("rows_g1", rows[1], BF16, "r"))
         c = full("c")
         nc.vector.tensor_tensor(c[:], dealt(c0), size_sb[:], ALU.mult)
         pv, tau = full("pv"), col("tau")
-        nc.vector.scalar_tensor_tensor(pv[:], pin[:], 1.0, vn[:], ALU.mult, ALU.mult, accum_out=tau[:])
+        nc.vector.scalar_tensor_tensor(pv[:], p[:], niz[:], vn[:], ALU.mult, ALU.mult, accum_out=tau[:])
         pcn, ns1 = full("pcn"), col("ns1")
-        nc.vector.scalar_tensor_tensor(pcn[:], pin[:], 1.0, c[:], ALU.mult, ALU.mult, accum_out=ns1[:])
-        turn_block(3, gather("rows_g3", rows[3], BF16, "vn"))
-        mass, kpn, mu = pag("mass"), pag("kpn"), pag("mu")
+        nc.vector.scalar_tensor_tensor(pcn[:], p[:], niz[:], c[:], ALU.mult, ALU.mult, accum_out=ns1[:])
+        turn_block(2, gather("rows_g2", rows[2], BF16, "vn"))
+        mass, lean_tau = pag("mass"), pag("lean_tau")
         nc.scalar.activation(mass[:], pn_page[:], ACT.Copy, scale=niz[:])
-        nc.vector.scalar_tensor_tensor(mu[:], kn[:], tau[:], ln[:], ALU.mult, ALU.add)
+        nc.scalar.activation(lean_tau[:], lean[:], ACT.Identity, bias=tau[:], scale=1.0 / PAGE)
         pcn_page = pag("pcn_page")
         nc.vector.tensor_reduce(pcn_page[:], pages_of(pcn), AX.XY, ALU.add)
         x, cov = full("x"), col("cov")
         nc.vector.scalar_tensor_tensor(x[:], c[:], ns1[:], pv[:], ALU.add, ALU.mult, accum_out=cov[:])
+        kt_codes = sbt("kt_codes", [P, D], U32, "c")
+        kt_plane = sbt("kt_plane", [P, D], U8)
+
+        def quantise_turned(h):
+            cols = slice(h * D // 2, (h + 1) * D // 2)
+            nc.vector.quantize_mx(out=kt_codes[:, cols].bitcast(FP8X4), scales=kt_plane[:, cols],
+                                  in_=kt_in[h][:].rearrange("p d t -> p (d t)"))
+
         y_page, pre, x_page = pag("y_page"), pag("pre"), pag("x_page")
         nc.vector.scalar_tensor_tensor(y_page[:], mass[:], ns1[:], pcn_page[:], ALU.mult, ALU.subtract)
-        nc.vector.scalar_tensor_tensor(kpn[:], mass[:], 1.0 / PAGE, kn[:], ALU.mult, ALU.mult)
-        nc.vector.scalar_tensor_tensor(pre[:], y_page[:], 1.0 / PAGE, mu[:], ALU.mult, ALU.mult)
+        quantise_turned(0)
+        nc.vector.tensor_tensor(pre[:], y_page[:], lean_tau[:], ALU.mult)
         nc.vector.tensor_reduce(x_page[:], pages_of(x), AX.XY, ALU.add)
-        tns, term_c, term_s, term_cov = col("tns"), full("term_c"), full("term_s"), full("term_cov")
-        nc.scalar.activation(tns[:], ns1[:], ACT.Copy, scale=tau[:])
+        tns, tns_z, weight, term_c, term_p = col("tns"), col("tns_z"), col("weight"), full("term_c"), full("term_p")
         nc.scalar.activation(term_c[:], pcn[:], ACT.Copy, scale=tau[:])
-        nc.scalar.activation(term_s[:], pin[:], ACT.Copy, scale=tns[:])
-        nc.scalar.activation(term_cov[:], pin[:], ACT.Copy, scale=cov[:])
-        early = sbt("early", [P, PAGES, PACK], F32)
-        late = sbt("late", [P, PAGES, PACK], F32)
-        nc.vector.scalar_tensor_tensor(early[:], by_quarter_page(kpn), cov[:], by_quarter_page(pre), ALU.mult, ALU.add)
-        nc.vector.scalar_tensor_tensor(late[:], by_quarter_page(x_page), -1.0 / PAGE, by_quarter_page(kn), ALU.mult, ALU.mult)
+        nc.scalar.activation(tns[:], ns1[:], ACT.Copy, scale=tau[:])
+        nc.scalar.activation(tns_z[:], tns[:], ACT.Copy, scale=niz[:])
+        nc.scalar.activation(weight[:], cov[:], ACT.Identity, bias=tns_z[:], scale=niz[:])
+        nc.scalar.activation(term_p[:], p[:], ACT.Copy, scale=weight[:])
+        early, late = pag("early"), pag("late")
+        term_g = sbt("term_g", [P, PAGES, PACK], F32)
+        nc.vector.scalar_tensor_tensor(early[:], mass[:], cov[:], pre[:], ALU.mult, ALU.add)
+        nc.vector.tensor_tensor(late[:], early[:], x_page[:], ALU.subtract)
+        nc.vector.scalar_tensor_tensor(term_g[:], by_quarter_page(late), 1.0 / PAGE, by_quarter_page(kn), ALU.mult, ALU.mult)
 
         g_t = ps.tile([P, PACK, Q], F32, name="g_t")
-        terms = [lambda t: term_c[:, t, :], lambda t: term_s[:, t, :], lambda t: x[:, t, :],
-                 lambda t: term_cov[:, t, :],
-                 lambda t: early[:].rearrange("q g u -> q (g u)"), lambda t: late[:].rearrange("q g u -> q (g u)")]
+        terms = [lambda t: term_c[:, t, :], lambda t: x[:, t, :], lambda t: term_p[:, t, :],
+                 lambda t: term_g[:].rearrange("q g u -> q (g u)")]
         for n, term in enumerate(terms):
             for t in range(PACK):
                 nc.tensor.matmul(g_t[:, t, :], term(t), ident[:], is_transpose=True,
                                  start=(n == 0 and t == 0), stop=(n == len(terms) - 1 and t == PACK - 1))
+        turn_block(3, gather("rows_g3", rows[3], BF16, "late"))
         g_in = sbt("g_in", [P, Q, PACK], BF16)
         nc.vector.tensor_tensor(g_in[:], g_t[:].rearrange("p t q -> p q t"),
                                 fs_c[:].unsqueeze(1).broadcast_to([P, Q, PACK]), ALU.mult)
         g_codes = sbt("g_codes", [P, Q], U32)
         g_plane = sbt("g_plane", [P, Q], U8)
         nc.vector.quantize_mx(out=g_codes[:].bitcast(FP8X4), scales=g_plane[:], in_=g_in[:].rearrange("p q t -> p (q t)"))
+
+        quantise_turned(1)
 
         half = D // 2
         for h, tag in enumerate(("a", "ta")):

@@ -55,6 +55,8 @@ def tile_attend_hvpagegate_q_kernel(tc, query, keys_words, keys_scales, th, stee
         v_scales = sbt("v_scales", [P, T], U8)
         nc.vector.memset(k_scales[:].bitcast(I32), 0)
         nc.vector.memset(v_scales[:].bitcast(I32), 0)
+        size_row = sbt("size_row", [P, SLOTS], F32)
+        nc.vector.memset(size_row[:], 0.0)
         warm = sbt("warm", [P, 1], F32)
         nc.vector.memset(warm[:], 0.0)
         warm2 = sbt("warm2", [P, 1], F32)
@@ -76,7 +78,6 @@ def tile_attend_hvpagegate_q_kernel(tc, query, keys_words, keys_scales, th, stee
         load_scales(k_scales, keys_scales)
         steep_c = sbt("steep_c", [P, 1], F32)
         th_c = sbt("th_c", [P, 1], F32)
-        size_c = sbt("size_c", [P, PACK], F32)
         fs_c = sbt("fs_c", [P, PACK], F32)
         rows = [sbt("rows%d" % j, [P, T], F32) for j in range(D // P)]
 
@@ -84,12 +85,12 @@ def tile_attend_hvpagegate_q_kernel(tc, query, keys_words, keys_scales, th, stee
             nc.sync.dma_start(out=rows[j][:], in_=keyrows[j * P:(j + 1) * P, :])
 
         nc.sync.dma_start(out=v_words[:].bitcast(I32), in_=vals_words[0].bitcast(I32))
+        go_raw = load_rows("go_raw", gout)
         nc.sync.dma_start(out=th_c[:], in_=th)
         nc.sync.dma_start(out=steep_c[:], in_=steep)
-        go_raw = load_rows("go_raw", gout)
-        load_scales(v_scales, vals_scales)
         load_block(0)
-        nc.sync.dma_start(out=size_c[:], in_=size.rearrange("o (m t) -> (o m) t", t=PACK))
+        load_scales(v_scales, vals_scales)
+        nc.sync.dma_start(out=size_row[0:1, :], in_=size)
         for j in range(1, D // P):
             load_block(j)
         nc.sync.dma_start(out=fs_c[:], in_=fs.rearrange("o (m t) -> (o m) t", t=PACK))
@@ -129,11 +130,11 @@ def tile_attend_hvpagegate_q_kernel(tc, query, keys_words, keys_scales, th, stee
         def col(name):
             return sbt(name, [P, 1], F32)
 
-        def pag(name):
-            return sbt(name, [P, PAGES], F32)
+        def pag(name, tag=None):
+            return sbt(name, [P, PAGES], F32, tag)
 
-        def full(name):
-            return sbt(name, [P, PACK, P], F32)
+        def full(name, tag=None):
+            return sbt(name, [P, PACK, P], F32, tag)
 
         kt_in = [sbt("kt_in%d" % h, [P, D // 2, PACK], BF16) for h in range(2)]
 
@@ -154,7 +155,7 @@ def tile_attend_hvpagegate_q_kernel(tc, query, keys_words, keys_scales, th, stee
                 nc.tensor.transpose(turned[:, u, :], words[:, u:SLOTS // 2:2], ident[:])
             nc.scalar.copy(kt_in[j // 2][:, (j % 2) * P:(j % 2 + 1) * P, :].bitcast(F32), turned[:].rearrange("p u d -> p d u"))
 
-        vg_words = gather("vg_words", v_words, U16, "q_woven")
+        vg_words = gather("vg_words", v_words, U16)
         (go_mx,) = quantise_rows("go", [go_raw])
         sa, sta, nmax = pag("sa"), pag("sta"), col("nmax")
         nc.vector.tensor_reduce(sa[:], a[:].rearrange("q (g j) -> q g j", j=PAGE), AX.X, ALU.add)
@@ -166,46 +167,58 @@ def tile_attend_hvpagegate_q_kernel(tc, query, keys_words, keys_scales, th, stee
         nc.scalar.activation(den[:], e[:], ACT.Copy, bias=1.0)
         r = full("r")
         nc.scalar.activation(r[:], dealt(a), ACT.Exp, bias=nmax[:])
-        vg_scales = gather("vg_scales", v_scales, U8, "sa")
-        c0 = score("c0", go_mx, vg_words, vg_scales)
-        size_b = ps.tile([P, PACK, P], F32, name="size_b", tag="a")
-        for t in range(PACK):
-            nc.tensor.transpose(size_b[:, t, :], size_c[:, t:t + 1].to_broadcast([P, P]), ident[:])
-        size_sb = full("size_sb")
-        nc.scalar.copy(size_sb[:], size_b[:])
-        for j in range(SCALAR_BLOCKS):
-            turn_block(j, pick_block(j, cast_block(j)))
-        gt = pag("gt")
         nc.vector.tensor_reduce(sta[:], ta[:].rearrange("q (g j) -> q g j", j=PAGE), AX.X, ALU.add)
+        vg_scales = gather("vg_scales", v_scales, U8)
+        gt = pag("gt", "v_scales")
         nc.vector.reciprocal(gt[:], den[:])
-        r_page = pag("r_page")
-        nc.vector.tensor_reduce(r_page[:], pages_of(r), AX.XY, ALU.add)
-        kn, hn, lean, pn_page, nz, niz = pag("kn"), pag("hn"), pag("lean"), pag("pn_page"), col("nz"), col("niz")
+        kn = pag("kn")
         nc.vector.tensor_scalar(kn[:], gt[:], 1.0, steep_c[:], ALU.subtract, ALU.mult)
+        cast0 = cast_block(0)
+        tiles = SLOTS // P
+        size_t = ps.tile([P, tiles, P], F32, name="size_t", tag="g_t")
+        for u in range(tiles):
+            nc.tensor.transpose(size_t[:, u, :], size_row[:, u * P:(u + 1) * P], ident[:])
+        size_c = sbt("size_c", [P, tiles], F32)
+        nc.scalar.copy(size_c[:], size_t[:, :, 0])
+        c0_t = ps.tile([P, tiles, Q], F32, name="c0_t")
+        for u in range(tiles):
+            slots = slice(u * P, (u + 1) * P)
+            nc.tensor.matmul_mx(out=c0_t[:, u, :], lhsT=vg_words[:, slots].bitcast(FP4X4), lhsT_scale=vg_scales[:, slots],
+                                rhs=go_mx[0].bitcast(FP8X4), rhs_scale=go_mx[1], start=True, stop=True)
+        c_t = sbt("c_t", [P, tiles, Q], F32)
+        c = ps.tile([P, SLOTS], F32, name="c", tag="a")
+        for u in range(tiles):
+            nc.scalar.activation(c_t[:, u, :], c0_t[:, u, :], ACT.Copy, scale=size_c[:, u:u + 1])
+        for u in range(tiles):
+            nc.tensor.transpose(c[:, u * P:(u + 1) * P], c_t[:, u, :], ident[:])
+        turn_block(0, pick_block(0, cast0))
+        hn, lean, p_page, nz, niz = pag("hn"), pag("lean"), pag("p_page"), col("nz"), col("niz")
         p = full("p")
         nc.vector.tensor_tensor(four(p[:]), four(r[:]), by_page(gt), ALU.mult)
         nc.vector.scalar_tensor_tensor(hn[:], sta[:], 1.0 / PAGE, kn[:], ALU.mult, ALU.mult)
-        nc.vector.scalar_tensor_tensor(pn_page[:], r_page[:], -1.0, gt[:], ALU.mult, ALU.mult, accum_out=nz[:])
-        nc.vector.scalar_tensor_tensor(lean[:], sta[:], steep_c[:], gt[:], ALU.mult, ALU.mult)
+        nc.vector.tensor_reduce(p_page[:], pages_of(p), AX.XY, ALU.add)
         vn = full("vn")
         nc.vector.tensor_tensor(four(vn[:]), by_page(hn), four(dealt(ta)), ALU.subtract)
+        nc.vector.tensor_reduce(nz[:], p_page[:], AX.X, ALU.add, negate=True)
+        nc.vector.scalar_tensor_tensor(lean[:], sta[:], steep_c[:], gt[:], ALU.mult, ALU.mult)
         nc.vector.reciprocal(niz[:], nz[:])
-        turn_block(1, gather("rows_g1", rows[1], BF16, "r"))
-        c = full("c")
-        nc.vector.tensor_tensor(c[:], dealt(c0), size_sb[:], ALU.mult)
-        pv, tau = full("pv"), col("tau")
-        nc.vector.scalar_tensor_tensor(pv[:], p[:], niz[:], vn[:], ALU.mult, ALU.mult, accum_out=tau[:])
+        turn_block(1, gather("rows_g1", rows[1], BF16))
         pcn, ns1 = full("pcn"), col("ns1")
-        nc.vector.scalar_tensor_tensor(pcn[:], p[:], niz[:], c[:], ALU.mult, ALU.mult, accum_out=ns1[:])
-        turn_block(2, gather("rows_g2", rows[2], BF16, "vn"))
-        mass, lean_tau = pag("mass"), pag("lean_tau")
-        nc.scalar.activation(mass[:], pn_page[:], ACT.Copy, scale=niz[:])
-        nc.scalar.activation(lean_tau[:], lean[:], ACT.Identity, bias=tau[:], scale=1.0 / PAGE)
-        pcn_page = pag("pcn_page")
-        nc.vector.tensor_reduce(pcn_page[:], pages_of(pcn), AX.XY, ALU.add)
+        nc.vector.scalar_tensor_tensor(pcn[:], p[:], niz[:], dealt(c), ALU.mult, ALU.mult, accum_out=ns1[:])
+        pv, tau = full("pv", "rows1"), col("tau")
+        nc.vector.scalar_tensor_tensor(pv[:], p[:], niz[:], vn[:], ALU.mult, ALU.mult, accum_out=tau[:])
+        turn_block(2, gather("rows_g2", rows[2], BF16))
+        side = sbt("side", [P, 2 * PAGES + 2], F32, "nmax")
+        massn, lean_tau = side[:, 0:PAGES], side[:, PAGES:2 * PAGES]
+        tau_z, tns_z = [side[:, 2 * PAGES + i:2 * PAGES + i + 1] for i in range(2)]
+        nc.scalar.activation(massn, p_page[:], ACT.Copy, scale=niz[:])
+        nc.scalar.activation(lean_tau, lean[:], ACT.Identity, bias=tau[:], scale=1.0 / PAGE)
+        nc.scalar.activation(tau_z, tau[:], ACT.Copy, scale=niz[:])
         x, cov = full("x"), col("cov")
-        nc.vector.scalar_tensor_tensor(x[:], c[:], ns1[:], pv[:], ALU.add, ALU.mult, accum_out=cov[:])
-        kt_codes = sbt("kt_codes", [P, D], U32, "c")
+        nc.vector.scalar_tensor_tensor(x[:], dealt(c), ns1[:], pv[:], ALU.add, ALU.mult, accum_out=cov[:])
+        pcn_page = pag("pcn_page", "rows2")
+        nc.vector.tensor_reduce(pcn_page[:], pages_of(pcn), AX.XY, ALU.add)
+        kt_codes = sbt("kt_codes", [P, D], U32, "rows1")
         kt_plane = sbt("kt_plane", [P, D], U8)
 
         def quantise_turned(h):
@@ -214,21 +227,20 @@ def tile_attend_hvpagegate_q_kernel(tc, query, keys_words, keys_scales, th, stee
                                   in_=kt_in[h][:].rearrange("p d t -> p (d t)"))
 
         y_page, pre, x_page = pag("y_page"), pag("pre"), pag("x_page")
-        nc.vector.scalar_tensor_tensor(y_page[:], mass[:], ns1[:], pcn_page[:], ALU.mult, ALU.subtract)
+        nc.vector.scalar_tensor_tensor(y_page[:], massn, ns1[:], pcn_page[:], ALU.mult, ALU.add)
         quantise_turned(0)
-        nc.vector.tensor_tensor(pre[:], y_page[:], lean_tau[:], ALU.mult)
+        nc.vector.tensor_tensor(pre[:], y_page[:], lean_tau, ALU.mult)
         nc.vector.tensor_reduce(x_page[:], pages_of(x), AX.XY, ALU.add)
-        tns, tns_z, weight, term_c, term_p = col("tns"), col("tns_z"), col("weight"), full("term_c"), full("term_p")
+        weight, term_c, term_p = col("weight"), full("term_c", "rows_g0"), full("term_p")
+        nc.scalar.activation(tns_z, ns1[:], ACT.Copy, scale=tau_z)
         nc.scalar.activation(term_c[:], pcn[:], ACT.Copy, scale=tau[:])
-        nc.scalar.activation(tns[:], ns1[:], ACT.Copy, scale=tau[:])
-        nc.scalar.activation(tns_z[:], tns[:], ACT.Copy, scale=niz[:])
-        nc.scalar.activation(weight[:], cov[:], ACT.Identity, bias=tns_z[:], scale=niz[:])
+        nc.scalar.activation(weight[:], cov[:], ACT.Identity, bias=tns_z, scale=niz[:])
         nc.scalar.activation(term_p[:], p[:], ACT.Copy, scale=weight[:])
         early, late = pag("early"), pag("late")
         term_g = sbt("term_g", [P, PAGES, PACK], F32)
-        nc.vector.scalar_tensor_tensor(early[:], mass[:], cov[:], pre[:], ALU.mult, ALU.add)
-        nc.vector.tensor_tensor(late[:], early[:], x_page[:], ALU.subtract)
-        nc.vector.scalar_tensor_tensor(term_g[:], by_quarter_page(late), 1.0 / PAGE, by_quarter_page(kn), ALU.mult, ALU.mult)
+        nc.vector.scalar_tensor_tensor(early[:], massn, cov[:], pre[:], ALU.mult, ALU.add)
+        nc.vector.tensor_tensor(late[:], early[:], x_page[:], ALU.add)
+        nc.vector.scalar_tensor_tensor(term_g[:], by_quarter_page(late), -1.0 / PAGE, by_quarter_page(kn), ALU.mult, ALU.mult)
 
         g_t = ps.tile([P, PACK, Q], F32, name="g_t")
         terms = [lambda t: term_c[:, t, :], lambda t: x[:, t, :], lambda t: term_p[:, t, :],

@@ -20,7 +20,6 @@ FP4X4 = mybir.dt.float4_e2m1fn_x4
 ALU = mybir.AluOpType
 ACT = mybir.ActivationFunctionType
 AX = mybir.AxisListType
-SCALAR_BLOCKS = 1
 
 
 def tile_attend_hvpagegate_q_kernel(tc, query, keys_words, keys_scales, th, steep, gout, vals_words, vals_scales,
@@ -148,15 +147,18 @@ def tile_attend_hvpagegate_q_kernel(tc, query, keys_words, keys_scales, th, stee
             nc.scalar.activation(got[:], cast[:].indirect(offsets[:]), ACT.Copy)
             return got
 
-        def turn_block(j, got):
+        def turn_block(got, turned):
             words = got[:].bitcast(F32)
-            turned = ps.tile([P, 2, P], F32, name="turned", bufs=2)
             for u in range(2):
                 nc.tensor.transpose(turned[:, u, :], words[:, u:SLOTS // 2:2], ident[:])
-            nc.scalar.copy(kt_in[j // 2][:, (j % 2) * P:(j % 2 + 1) * P, :].bitcast(F32), turned[:].rearrange("p u d -> p d u"))
+
+        def weave_block(j, turned):
+            nc.scalar.copy(kt_in[j // 2][:, (j % 2) * P:(j % 2 + 1) * P, :].bitcast(F32), turned.rearrange("p u d -> p d u"))
 
         vg_words = gather("vg_words", v_words, U16)
         (go_mx,) = quantise_rows("go", [go_raw])
+        slope = col("slope")
+        nc.scalar.activation(slope[:], steep_c[:], ACT.Copy, scale=1.0 / PAGE)
         sa, sta, nmax = pag("sa"), pag("sta"), col("nmax")
         nc.vector.tensor_reduce(sa[:], a[:].rearrange("q (g j) -> q g j", j=PAGE), AX.X, ALU.add)
         nc.vector.tensor_reduce(nmax[:], a[:], AX.X, ALU.max, negate=True)
@@ -172,7 +174,7 @@ def tile_attend_hvpagegate_q_kernel(tc, query, keys_words, keys_scales, th, stee
         gt = pag("gt", "v_scales")
         nc.vector.reciprocal(gt[:], den[:])
         kn = pag("kn")
-        nc.vector.tensor_scalar(kn[:], gt[:], 1.0, steep_c[:], ALU.subtract, ALU.mult)
+        nc.vector.tensor_scalar(kn[:], gt[:], 1.0, slope[:], ALU.subtract, ALU.mult)
         cast0 = cast_block(0)
         tiles = SLOTS // P
         size_t = ps.tile([P, tiles, P], F32, name="size_t", tag="g_t")
@@ -191,34 +193,57 @@ def tile_attend_hvpagegate_q_kernel(tc, query, keys_words, keys_scales, th, stee
             nc.scalar.activation(c_t[:, u, :], c0_t[:, u, :], ACT.Copy, scale=size_c[:, u:u + 1])
         for u in range(tiles):
             nc.tensor.transpose(c[:, u * P:(u + 1) * P], c_t[:, u, :], ident[:])
-        turn_block(0, pick_block(0, cast0))
+        turned01 = ps.tile([P, 2, 2, P], F32, name="turned01", tag="turned", bufs=2)
+        turn_block(pick_block(0, cast0), turned01[:, 0])
         hn, lean, p_page, nz, niz = pag("hn"), pag("lean"), pag("p_page"), col("nz"), col("niz")
         p = full("p")
         nc.vector.tensor_tensor(four(p[:]), four(r[:]), by_page(gt), ALU.mult)
-        nc.vector.scalar_tensor_tensor(hn[:], sta[:], 1.0 / PAGE, kn[:], ALU.mult, ALU.mult)
+        nc.vector.tensor_tensor(hn[:], sta[:], kn[:], ALU.mult)
         nc.vector.tensor_reduce(p_page[:], pages_of(p), AX.XY, ALU.add)
         vn = full("vn")
         nc.vector.tensor_tensor(four(vn[:]), by_page(hn), four(dealt(ta)), ALU.subtract)
         nc.vector.tensor_reduce(nz[:], p_page[:], AX.X, ALU.add, negate=True)
-        nc.vector.scalar_tensor_tensor(lean[:], sta[:], steep_c[:], gt[:], ALU.mult, ALU.mult)
+        nc.vector.scalar_tensor_tensor(lean[:], sta[:], slope[:], gt[:], ALU.mult, ALU.mult)
         nc.vector.reciprocal(niz[:], nz[:])
-        turn_block(1, gather("rows_g1", rows[1], BF16))
+        massn = pag("massn")
+        turn_block(gather("rows_g1", rows[1], BF16), turned01[:, 1])
+        nc.scalar.copy(kt_in[0][:].bitcast(F32).rearrange("p (b d) u -> p b d u", b=2),
+                       turned01[:].rearrange("p b u d -> p b d u"))
+        nc.vector.tensor_scalar(massn[:], p_page[:], niz[:], None, ALU.mult)
         pcn, ns1 = full("pcn"), col("ns1")
         nc.vector.scalar_tensor_tensor(pcn[:], p[:], niz[:], dealt(c), ALU.mult, ALU.mult, accum_out=ns1[:])
         pv, tau = full("pv", "rows1"), col("tau")
         nc.vector.scalar_tensor_tensor(pv[:], p[:], niz[:], vn[:], ALU.mult, ALU.mult, accum_out=tau[:])
-        turn_block(2, gather("rows_g2", rows[2], BF16))
-        side = sbt("side", [P, 2 * PAGES + 2], F32, "nmax")
-        massn, lean_tau = side[:, 0:PAGES], side[:, PAGES:2 * PAGES]
-        tau_z, tns_z = [side[:, 2 * PAGES + i:2 * PAGES + i + 1] for i in range(2)]
-        nc.scalar.activation(massn, p_page[:], ACT.Copy, scale=niz[:])
-        nc.scalar.activation(lean_tau, lean[:], ACT.Identity, bias=tau[:], scale=1.0 / PAGE)
+        turned2 = ps.tile([P, 2, P], F32, name="turned2", tag="turned", bufs=2)
+        turn_block(gather("rows_g2", rows[2], BF16), turned2[:])
+        side = sbt("side", [P, 2], F32, "nmax")
+        tau_z, tns_z = side[:, 0:1], side[:, 1:2]
         nc.scalar.activation(tau_z, tau[:], ACT.Copy, scale=niz[:])
         x, cov = full("x"), col("cov")
         nc.vector.scalar_tensor_tensor(x[:], dealt(c), ns1[:], pv[:], ALU.add, ALU.mult, accum_out=cov[:])
         pcn_page = pag("pcn_page", "rows2")
         nc.vector.tensor_reduce(pcn_page[:], pages_of(pcn), AX.XY, ALU.add)
-        kt_codes = sbt("kt_codes", [P, D], U32, "rows1")
+        y_page, pre, x_page, early = pag("y_page"), pag("pre"), pag("x_page"), pag("early")
+        nc.vector.tensor_reduce(x_page[:], pages_of(x), AX.XY, ALU.add)
+        nc.vector.scalar_tensor_tensor(y_page[:], massn[:], ns1[:], pcn_page[:], ALU.mult, ALU.add)
+        nc.vector.scalar_tensor_tensor(early[:], massn[:], cov[:], x_page[:], ALU.mult, ALU.add)
+        nc.vector.scalar_tensor_tensor(pre[:], lean[:], tau[:], y_page[:], ALU.add, ALU.mult)
+        weight, term_c, term_p = col("weight"), full("term_c", "rows_g0"), full("term_p")
+        nc.scalar.activation(tns_z, ns1[:], ACT.Copy, scale=tau_z)
+        nc.scalar.activation(term_c[:], pcn[:], ACT.Copy, scale=tau[:])
+        nc.scalar.activation(weight[:], cov[:], ACT.Identity, bias=tns_z, scale=niz[:])
+        nc.scalar.activation(term_p[:], p[:], ACT.Copy, scale=weight[:])
+        weave_block(2, turned2[:])
+        got3 = sbt("rows_g3", [P, SLOTS], BF16)
+        mid = 3 * SLOTS // 4
+        nc.vector.tensor_copy(got3[:, :mid], rows[3][:].indirect(offsets[:, :mid // 16]))
+        late = got3[:, mid:mid + 2 * PAGES].bitcast(F32)
+        term_g = sbt("term_g", [P, PAGES, PACK], F32)
+        nc.vector.tensor_tensor(late, early[:], pre[:], ALU.add)
+        nc.vector.scalar_tensor_tensor(term_g[:], late.unsqueeze(2).broadcast_to([P, PAGES, PACK]), -1.0,
+                                       by_quarter_page(kn), ALU.mult, ALU.mult)
+
+        kt_codes = sbt("kt_codes", [P, D], U32, "kn")
         kt_plane = sbt("kt_plane", [P, D], U8)
 
         def quantise_turned(h):
@@ -226,30 +251,18 @@ def tile_attend_hvpagegate_q_kernel(tc, query, keys_words, keys_scales, th, stee
             nc.vector.quantize_mx(out=kt_codes[:, cols].bitcast(FP8X4), scales=kt_plane[:, cols],
                                   in_=kt_in[h][:].rearrange("p d t -> p (d t)"))
 
-        y_page, pre, x_page = pag("y_page"), pag("pre"), pag("x_page")
-        nc.vector.scalar_tensor_tensor(y_page[:], massn, ns1[:], pcn_page[:], ALU.mult, ALU.add)
-        quantise_turned(0)
-        nc.vector.tensor_tensor(pre[:], y_page[:], lean_tau, ALU.mult)
-        nc.vector.tensor_reduce(x_page[:], pages_of(x), AX.XY, ALU.add)
-        weight, term_c, term_p = col("weight"), full("term_c", "rows_g0"), full("term_p")
-        nc.scalar.activation(tns_z, ns1[:], ACT.Copy, scale=tau_z)
-        nc.scalar.activation(term_c[:], pcn[:], ACT.Copy, scale=tau[:])
-        nc.scalar.activation(weight[:], cov[:], ACT.Identity, bias=tns_z, scale=niz[:])
-        nc.scalar.activation(term_p[:], p[:], ACT.Copy, scale=weight[:])
-        early, late = pag("early"), pag("late")
-        term_g = sbt("term_g", [P, PAGES, PACK], F32)
-        nc.vector.scalar_tensor_tensor(early[:], massn, cov[:], pre[:], ALU.mult, ALU.add)
-        nc.vector.tensor_tensor(late[:], early[:], x_page[:], ALU.add)
-        nc.vector.scalar_tensor_tensor(term_g[:], by_quarter_page(late), -1.0 / PAGE, by_quarter_page(kn), ALU.mult, ALU.mult)
-
         g_t = ps.tile([P, PACK, Q], F32, name="g_t")
-        terms = [lambda t: term_c[:, t, :], lambda t: x[:, t, :], lambda t: term_p[:, t, :],
+        terms = [lambda t: x[:, t, :], lambda t: term_c[:, t, :], lambda t: term_p[:, t, :],
                  lambda t: term_g[:].rearrange("q g u -> q (g u)")]
         for n, term in enumerate(terms):
             for t in range(PACK):
                 nc.tensor.matmul(g_t[:, t, :], term(t), ident[:], is_transpose=True,
                                  start=(n == 0 and t == 0), stop=(n == len(terms) - 1 and t == PACK - 1))
-        turn_block(3, gather("rows_g3", rows[3], BF16, "late"))
+        turned3 = ps.tile([P, 2, P], F32, name="turned3", tag="turned", bufs=2)
+        nc.vector.tensor_copy(got3[:, mid:], rows[3][:].indirect(offsets[:, mid // 16:]))
+        quantise_turned(0)
+        turn_block(got3, turned3[:])
+        weave_block(3, turned3[:])
         g_in = sbt("g_in", [P, Q, PACK], BF16)
         nc.vector.tensor_tensor(g_in[:], g_t[:].rearrange("p t q -> p q t"),
                                 fs_c[:].unsqueeze(1).broadcast_to([P, Q, PACK]), ALU.mult)

from contextlib import ExitStack

import concourse.mybir as mybir
from concourse.masks import make_identity

D, E, T, SLOTS, Q, PAGES = 512, 512, 2048, 512, 128, 32
FLOPS = 2 * Q * SLOTS * (2 * D + E) + 2 * Q * SLOTS * D

P = 128
PACK = 4
PAGE = SLOTS // PAGES
F32 = mybir.dt.float32
BF16 = mybir.dt.bfloat16
I32 = mybir.dt.int32
U32 = mybir.dt.uint32
U16 = mybir.dt.uint16
U8 = mybir.dt.uint8
FP8X4 = mybir.dt.float8_e4m3fn_x4
FP4X4 = mybir.dt.float4_e2m1fn_x4
ALU = mybir.AluOpType
ACT = mybir.ActivationFunctionType
AX = mybir.AxisListType


def tile_attend_hvpagegate_q_kernel(tc, query, keys_words, keys_scales, th, steep, gout, vals_words, vals_scales,
                                     size, dquery, fs, keyrows, res, offs, out):
    nc = tc.nc
    with ExitStack() as ctx:
        sb = ctx.enter_context(tc.tile_pool(name="sb", bufs=1))
        ps = ctx.enter_context(tc.psum_pool(name="ps", bufs=1))

        def sbt(name, shape, dtype, tag=None):
            return sb.tile(shape, dtype, name=name, tag=tag or name, align_bytes=64)

        def by_page(t):
            return t[:].unsqueeze(1).unsqueeze(3).broadcast_to([P, PACK, PAGES, PACK])

        def by_quarter_page(t):
            return t[:].unsqueeze(2).broadcast_to([P, PAGES, PACK])

        def dealt(bank):
            return bank[:].rearrange("q (m t) -> q t m", t=PACK)

        def pages_of(t):
            return t[:].rearrange("q t (g u) -> q g t u", u=PACK)

        def four(t):
            return t.rearrange("q t (g u) -> q t g u", u=PACK)

        offsets = sb.tile([P, SLOTS // 16], U16, name="offsets")
        k_words = sbt("k_words", [P, T], U16)
        k_scales = sbt("k_scales", [P, T], U8)
        v_words = sbt("v_words", [P, T], U16)
        v_scales = sbt("v_scales", [P, T], U8)
        nc.vector.memset(k_scales[:].bitcast(I32), 0)
        nc.vector.memset(v_scales[:].bitcast(I32), 0)
        size_row = sbt("size_row", [P, SLOTS], F32)
        nc.vector.memset(size_row[:], 0.0)
        warm = sbt("warm", [P, 1], F32)
        nc.vector.memset(warm[:], 0.0)
        warm2 = sbt("warm2", [P, 1], F32)
        nc.scalar.activation(warm2[:], warm[:], ACT.Exp)

        def load_rows(name, src):
            raw = sbt(name, [P, PACK, Q], F32)
            nc.sync.dma_start(out=raw[:], in_=src.rearrange("(p j) q -> p j q", j=PACK))
            return raw

        def load_scales(plane, src):
            for r in range(4):
                nc.sync.dma_start(out=plane[r:P:32, :].bitcast(I32), in_=src[0, r:16:4, :].bitcast(I32))

        nc.sync.dma_start(offsets[:], offs)
        nc.sync.dma_start(out=k_words[:].bitcast(I32), in_=keys_words[0].bitcast(I32))
        q_raw = load_rows("q_raw", query)
        dq_raw = load_rows("dq_raw", dquery)
        load_scales(k_scales, keys_scales)
        steep_c = sbt("steep_c", [P, 1], F32)
        th_c = sbt("th_c", [P, 1], F32)
        fs_c = sbt("fs_c", [P, PACK], F32)
        rows = [sbt("rows%d" % j, [P, T], F32) for j in range(D // P)]

        def load_block(j):
            nc.sync.dma_start(out=rows[j][:], in_=keyrows[j * P:(j + 1) * P, :])

        nc.sync.dma_start(out=v_words[:].bitcast(I32), in_=vals_words[0].bitcast(I32))
        go_raw = load_rows("go_raw", gout)
        nc.sync.dma_start(out=th_c[:], in_=th)
        nc.sync.dma_start(out=steep_c[:], in_=steep)
        load_block(0)
        load_scales(v_scales, vals_scales)
        nc.sync.dma_start(out=size_row[0:1, :], in_=size)
        for j in range(1, D // P):
            load_block(j)
        nc.sync.dma_start(out=fs_c[:], in_=fs.rearrange("o (m t) -> (o m) t", t=PACK))
        res_sb = sbt("res_sb", [P, D], F32)
        nc.sync.dma_start(out=res_sb[:], in_=res)
        ident = sbt("ident", [P, P], F32)
        make_identity(nc, ident[:])

        def quantise_rows(name, raws):
            n = len(raws)
            woven = sbt(name + "_woven", [P, n * Q, PACK], BF16)
            for i, raw in enumerate(raws):
                nc.scalar.copy(woven[:, i * Q:(i + 1) * Q, :], raw[:].rearrange("p j q -> p q j"))
            codes = sbt(name + "_codes", [P, n * Q], U32)
            plane = sbt(name + "_plane", [P, n * Q], U8)
            nc.vector.quantize_mx(out=codes[:].bitcast(FP8X4), scales=plane[:],
                                  in_=woven[:].rearrange("p q j -> p (q j)"))
            return [(codes[:, i * Q:(i + 1) * Q], plane[:, i * Q:(i + 1) * Q]) for i in range(n)]

        def gather(name, window, dtype, tag=None):
            got = sbt(name, [P, SLOTS], dtype, tag)
            nc.vector.tensor_copy(got[:], window[:].indirect(offsets[:]))
            return got

        def score(name, rows_mx, words, plane):
            bank = ps.tile([P, SLOTS], F32, name=name)
            nc.tensor.matmul_mx(out=bank[:], lhsT=rows_mx[0].bitcast(FP8X4), lhsT_scale=rows_mx[1],
                                rhs=words[:].bitcast(FP4X4), rhs_scale=plane[:], start=True, stop=True)
            return bank

        kg_words = gather("kg_words", k_words, U16)
        kg_scales = gather("kg_scales", k_scales, U8)
        q_mx, dq_mx = quantise_rows("q", [q_raw, dq_raw])
        a = score("a", q_mx, kg_words, kg_scales)
        ta = score("ta", dq_mx, kg_words, kg_scales)

        def col(name):
            return sbt(name, [P, 1], F32)

        def pag(name, tag=None):
            return sbt(name, [P, PAGES], F32, tag)

        def full(name, tag=None):
            return sbt(name, [P, PACK, P], F32, tag)

        kt_in = [sbt("kt_in%d" % h, [P, D // 2, PACK], BF16) for h in range(2)]

        def cast_block(j):
            cast = sbt("rows_bf%d" % j, [P, T], BF16, "nmax")
            nc.scalar.activation(cast[:], rows[j][:], ACT.Copy)
            return cast

        def pick_block(j, cast):
            got = sbt("rows_g%d" % j, [P, SLOTS], BF16)
            nc.scalar.activation(got[:], cast[:].indirect(offsets[:]), ACT.Copy)
            return got

        def turn_block(got, turned):
            words = got[:].bitcast(F32)
            for u in range(2):
                nc.tensor.transpose(turned[:, u, :], words[:, u:SLOTS // 2:2], ident[:])

        def weave_block(j, turned):
            nc.scalar.copy(kt_in[j // 2][:, (j % 2) * P:(j % 2 + 1) * P, :].bitcast(F32), turned.rearrange("p u d -> p d u"))

        vg_words = gather("vg_words", v_words, U16)
        (go_mx,) = quantise_rows("go", [go_raw])
        slope = col("slope")
        nc.scalar.activation(slope[:], steep_c[:], ACT.Copy, scale=1.0 / PAGE)
        sa, sta, nmax = pag("sa"), pag("sta"), col("nmax")
        nc.vector.tensor_reduce(sa[:], a[:].rearrange("q (g j) -> q g j", j=PAGE), AX.X, ALU.add)
        nc.vector.tensor_reduce(nmax[:], a[:], AX.X, ALU.max, negate=True)
        short, e = pag("short"), pag("e")
        den = pag("den")
        nc.scalar.activation(short[:], sa[:], ACT.Identity, bias=th_c[:], scale=-1.0 / PAGE)
        nc.scalar.activation(e[:], short[:], ACT.Exp, scale=steep_c[:])
        nc.scalar.activation(den[:], e[:], ACT.Copy, bias=1.0)
        r = full("r")
        nc.scalar.activation(r[:], dealt(a), ACT.Exp, bias=nmax[:])
        nc.vector.tensor_reduce(sta[:], ta[:].rearrange("q (g j) -> q g j", j=PAGE), AX.X, ALU.add)
        vg_scales = gather("vg_scales", v_scales, U8)
        gt = pag("gt", "v_scales")
        nc.vector.reciprocal(gt[:], den[:])
        kn = pag("kn")
        nc.vector.tensor_scalar(kn[:], gt[:], 1.0, slope[:], ALU.subtract, ALU.mult)
        cast0 = cast_block(0)
        tiles = SLOTS // P
        size_t = ps.tile([P, tiles, P], F32, name="size_t", tag="g_t")
        for u in range(tiles):
            nc.tensor.transpose(size_t[:, u, :], size_row[:, u * P:(u + 1) * P], ident[:])
        size_c = sbt("size_c", [P, tiles], F32)
        nc.scalar.copy(size_c[:], size_t[:, :, 0])
        c0_t = ps.tile([P, tiles, Q], F32, name="c0_t")
        for u in range(tiles):
            slots = slice(u * P, (u + 1) * P)
            nc.tensor.matmul_mx(out=c0_t[:, u, :], lhsT=vg_words[:, slots].bitcast(FP4X4), lhsT_scale=vg_scales[:, slots],
                                rhs=go_mx[0].bitcast(FP8X4), rhs_scale=go_mx[1], start=True, stop=True)
        c_t = sbt("c_t", [P, tiles, Q], F32)
        c = ps.tile([P, SLOTS], F32, name="c", tag="a")
        for u in range(tiles):
            nc.scalar.activation(c_t[:, u, :], c0_t[:, u, :], ACT.Copy, scale=size_c[:, u:u + 1])
        for u in range(tiles):
            nc.tensor.transpose(c[:, u * P:(u + 1) * P], c_t[:, u, :], ident[:])
        turned01 = ps.tile([P, 2, 2, P], F32, name="turned01", tag="turned", bufs=2)
        turn_block(pick_block(0, cast0), turned01[:, 0])
        hn, lean, p_page, nz, niz = pag("hn"), pag("lean"), pag("p_page"), col("nz"), col("niz")
        p = full("p")
        nc.vector.tensor_tensor(four(p[:]), four(r[:]), by_page(gt), ALU.mult)
        nc.vector.tensor_tensor(hn[:], sta[:], kn[:], ALU.mult)
        nc.vector.tensor_reduce(p_page[:], pages_of(p), AX.XY, ALU.add)
        vn = full("vn")
        nc.vector.tensor_tensor(four(vn[:]), by_page(hn), four(dealt(ta)), ALU.subtract)
        nc.vector.tensor_reduce(nz[:], p_page[:], AX.X, ALU.add, negate=True)
        nc.vector.scalar_tensor_tensor(lean[:], sta[:], slope[:], gt[:], ALU.mult, ALU.mult)
        nc.vector.reciprocal(niz[:], nz[:])
        massn = pag("massn")
        turn_block(gather("rows_g1", rows[1], BF16), turned01[:, 1])
        nc.scalar.copy(kt_in[0][:].bitcast(F32).rearrange("p (b d) u -> p b d u", b=2),
                       turned01[:].rearrange("p b u d -> p b d u"))
        nc.vector.tensor_scalar(massn[:], p_page[:], niz[:], None, ALU.mult)
        pcn, ns1 = full("pcn"), col("ns1")
        nc.vector.scalar_tensor_tensor(pcn[:], p[:], niz[:], dealt(c), ALU.mult, ALU.mult, accum_out=ns1[:])
        pv, tau = full("pv", "rows1"), col("tau")
        nc.vector.scalar_tensor_tensor(pv[:], p[:], niz[:], vn[:], ALU.mult, ALU.mult, accum_out=tau[:])
        turned2 = ps.tile([P, 2, P], F32, name="turned2", tag="turned", bufs=2)
        turn_block(gather("rows_g2", rows[2], BF16), turned2[:])
        side = sbt("side", [P, 2], F32, "nmax")
        tau_z, tns_z = side[:, 0:1], side[:, 1:2]
        nc.scalar.activation(tau_z, tau[:], ACT.Copy, scale=niz[:])
        x, cov = full("x"), col("cov")
        nc.vector.scalar_tensor_tensor(x[:], dealt(c), ns1[:], pv[:], ALU.add, ALU.mult, accum_out=cov[:])
        pcn_page = pag("pcn_page", "rows2")
        nc.vector.tensor_reduce(pcn_page[:], pages_of(pcn), AX.XY, ALU.add)
        y_page, pre, x_page, early = pag("y_page"), pag("pre"), pag("x_page"), pag("early")
        nc.vector.tensor_reduce(x_page[:], pages_of(x), AX.XY, ALU.add)
        nc.vector.scalar_tensor_tensor(y_page[:], massn[:], ns1[:], pcn_page[:], ALU.mult, ALU.add)
        nc.vector.scalar_tensor_tensor(early[:], massn[:], cov[:], x_page[:], ALU.mult, ALU.add)
        nc.vector.scalar_tensor_tensor(pre[:], lean[:], tau[:], y_page[:], ALU.add, ALU.mult)
        weight, term_c, term_p = col("weight"), full("term_c", "rows_g0"), full("term_p")
        nc.scalar.activation(tns_z, ns1[:], ACT.Copy, scale=tau_z)
        nc.scalar.activation(term_c[:], pcn[:], ACT.Copy, scale=tau[:])
        nc.scalar.activation(weight[:], cov[:], ACT.Identity, bias=tns_z, scale=niz[:])
        nc.scalar.activation(term_p[:], p[:], ACT.Copy, scale=weight[:])
        weave_block(2, turned2[:])
        got3 = sbt("rows_g3", [P, SLOTS], BF16)
        mid = 3 * SLOTS // 4
        nc.vector.tensor_copy(got3[:, :mid], rows[3][:].indirect(offsets[:, :mid // 16]))
        late = got3[:, mid:mid + 2 * PAGES].bitcast(F32)
        term_g = sbt("term_g", [P, PAGES, PACK], F32)
        nc.vector.tensor_tensor(late, early[:], pre[:], ALU.add)
        nc.vector.scalar_tensor_tensor(term_g[:], late.unsqueeze(2).broadcast_to([P, PAGES, PACK]), -1.0,
                                       by_quarter_page(kn), ALU.mult, ALU.mult)

        kt_codes = sbt("kt_codes", [P, D], U32, "kn")
        kt_plane = sbt("kt_plane", [P, D], U8)

        def quantise_turned(h):
            cols = slice(h * D // 2, (h + 1) * D // 2)
            nc.vector.quantize_mx(out=kt_codes[:, cols].bitcast(FP8X4), scales=kt_plane[:, cols],
                                  in_=kt_in[h][:].rearrange("p d t -> p (d t)"))

        g_t = ps.tile([P, PACK, Q], F32, name="g_t")
        terms = [lambda t: x[:, t, :], lambda t: term_c[:, t, :], lambda t: term_p[:, t, :],
                 lambda t: term_g[:].rearrange("q g u -> q (g u)")]
        for n, term in enumerate(terms):
            for t in range(PACK):
                nc.tensor.matmul(g_t[:, t, :], term(t), ident[:], is_transpose=True,
                                 start=(n == 0 and t == 0), stop=(n == len(terms) - 1 and t == PACK - 1))
        turned3 = ps.tile([P, 2, P], F32, name="turned3", tag="turned", bufs=2)
        nc.vector.tensor_copy(got3[:, mid:], rows[3][:].indirect(offsets[:, mid // 16:]))
        quantise_turned(0)
        turn_block(got3, turned3[:])
        weave_block(3, turned3[:])
        g_in = sbt("g_in", [P, Q, PACK], BF16)
        nc.vector.tensor_tensor(g_in[:], g_t[:].rearrange("p t q -> p q t"),
                                fs_c[:].unsqueeze(1).broadcast_to([P, Q, PACK]), ALU.mult)
        g_codes = sbt("g_codes", [P, Q], U32)
        g_plane = sbt("g_plane", [P, Q], U8)
        nc.vector.quantize_mx(out=g_codes[:].bitcast(FP8X4), scales=g_plane[:], in_=g_in[:].rearrange("p q t -> p (q t)"))

        quantise_turned(1)

        half = D // 2
        for h, tag in enumerate(("a", "ta")):
            cols = slice(h * half, (h + 1) * half)
            acc = ps.tile([P, half], F32, name="acc%d" % h, tag=tag)
            nc.tensor.matmul_mx(out=acc[:], lhsT=g_codes[:].bitcast(FP8X4), lhsT_scale=g_plane[:],
                                rhs=kt_codes[:, cols].bitcast(FP8X4), rhs_scale=kt_plane[:, cols], start=True, stop=True)
            done = sbt("done%d" % h, [P, half], F32)
            nc.vector.tensor_tensor(done[:], acc[:], res_sb[:, cols], ALU.add)
            nc.sync.dma_start(out=out[:, cols], in_=done[:])
